import numpy as np
import ml_dtypes


def mxq(x, axis, fmt="e4m3"):
    dtype, down = {"e4m3": (ml_dtypes.float8_e4m3fn, 7), "e5m2": (ml_dtypes.float8_e5m2, 14)}[fmt]
    v = np.moveaxis(np.asarray(x, np.float32).astype(ml_dtypes.bfloat16).astype(np.float64), axis, -1)
    blocks = v.reshape(v.shape[:-1] + (-1, 32))
    amax = np.abs(blocks).max(-1, keepdims=True)
    byte = np.maximum(np.where(amax > 0, np.frexp(amax)[1] - 1 + 127, 0) - down, 1)
    scale = np.exp2(byte - 127.0)
    codes = (blocks / scale).astype(np.float32).astype(dtype).astype(np.float64)
    return np.moveaxis((codes * scale).reshape(v.shape), -1, axis)


WIDE = False


def mx_kscale(k):
    if not WIDE:
        return np.ones(k)
    levels = np.array([30, -30])
    if k % 512:
        return np.exp2(np.random.permutation(np.resize(levels, k // 32))).repeat(32)
    a = np.empty((k // 512, 16))
    for p in range(k // 512):
        a[p, :8] = np.random.permutation(np.resize(levels, 8))
        for g in range(8):
            far = levels[np.abs(levels - a[p, g]) >= 10]
            a[p, g + 8] = far[np.random.randint(len(far))]
    return np.exp2(a.ravel()).repeat(32)


def f64(x):
    return np.asarray(x).astype(np.float64)


def striped(idx):
    return np.tile(np.asarray(idx).reshape(-1, 16).T, (8, 1)).astype(np.uint16)


def unstriped(offs):
    return offs[:16].T.reshape(-1).astype(np.int64)


E2M1 = np.array([0.0, 0.5, 1.0, 1.5, 2.0, 3.0, 4.0, 6.0, -0.0, -0.5, -1.0, -1.5, -2.0, -3.0, -4.0, -6.0])


def pack_weight(w, fmt):
    k, n = w.shape
    w = f64(np.asarray(w, np.float32).astype(ml_dtypes.bfloat16)).reshape(k // 32, 32, n)
    amax = np.abs(w).max(1)
    if fmt in ("e4m3", "e5m2"):
        byte = np.frexp(amax)[1] - 1 + 127 - (7 if fmt == "e4m3" else 14)
    else:
        mant, ex = np.frexp(amax / 6.0)
        byte = np.where(mant > 0.5, ex, ex - 1) + 127
    byte = np.clip(np.where(amax > 0, byte, 1), 1, 254)
    scaled = (w * np.exp2(127.0 - byte)[:, None, :]).reshape(k, n).astype(np.float32)
    by_word = np.ascontiguousarray(scaled.reshape(k // 512, 128, 4, n).transpose(0, 1, 3, 2))
    if fmt in ("e4m3", "e5m2"):
        words = by_word.astype(ml_dtypes.float8_e4m3fn if fmt == "e4m3" else ml_dtypes.float8_e5m2).view(np.uint8)
    else:
        c = by_word.astype(ml_dtypes.float4_e2m1fn).view(np.uint8) & 0xF
        words = (c[..., 0::2] | (c[..., 1::2] << 4)).reshape(k // 512, 128, 2 * n)
    return np.ascontiguousarray(words), np.ascontiguousarray(byte.astype(np.uint8).reshape(k // 512, 16, n))


def unpack_weight(words, scales, fmt):
    g, _, n = scales.shape
    words = np.ascontiguousarray(words).reshape(g, 128, n, -1)
    if fmt in ("e4m3", "e5m2"):
        vals = words.view(ml_dtypes.float8_e4m3fn if fmt == "e4m3" else ml_dtypes.float8_e5m2).astype(np.float64)
    else:
        nib = np.empty((g, 128, n, 4), np.uint8)
        nib[..., 0::2] = words & 0xF
        nib[..., 1::2] = words >> 4
        vals = E2M1[nib]
    vals = vals * np.repeat(np.exp2(scales.astype(np.float64) - 127.0), 8, axis=1)[..., None]
    return vals.transpose(0, 1, 3, 2).reshape(g * 512, n)


K, T, J, S, R, G, N = 1024, 1024, 384, 512, 512, 48, 256


def setup_inputs():
    n = np.random.standard_normal
    idx = np.random.permutation(T)[:J]
    idx2 = np.random.permutation(S)[:J]
    fk = mx_kscale(K)
    fr = mx_kscale(R)
    wp = pack_weight(n((K, R)) * 1 / np.sqrt(K) * fk[:, None] * fr, "e5m2")
    wbp = pack_weight(n((R, N)) * 1 / np.sqrt(R) / fr[:, None], "e5m2")
    return {
        "xa": (n((K, T))).astype(np.float32),
        "xb": (n((K, S))).astype(np.float32),
        "fk": (np.random.uniform(0.5, 2.0, (K, 1)) / fk[:, None]).astype(np.float32),
        "w_words": wp[0],
        "w_scales": wp[1],
        "wb_words": wbp[0],
        "wb_scales": wbp[1],
        "rs": (1.0 * n((J, N))).astype(np.float32),
        "offs": striped(idx),
        "offs2": striped(idx2),
    }


def reference(xa, xb, fk, w_words, w_scales, wb_words, wb_scales, rs, offs, offs2):
    idx = unstriped(offs)
    idx2 = unstriped(offs2)
    wu = unpack_weight(w_words, w_scales, "e5m2")
    wbu = unpack_weight(wb_words, wb_scales, "e5m2")
    u = f64(xa)[:, idx] * f64(xb)[:, idx2] * f64(fk)
    uq = mxq(u, 0, "e4m3")
    a = wu.T @ uq
    m1 = a.reshape(R, G, J // G).mean(axis=2)
    m2 = np.repeat(m1, J // G, axis=1)
    hid = a - m2
    hidq = mxq(hid, 0, "e4m3")
    p = hidq.T @ wbu
    mn = np.mean(np.abs(p), axis=1, keepdims=True)
    y = np.maximum(p - mn, 0.0) - 0.3 * f64(rs)
    return y

@@ -1,0 +1,227 @@
+from contextlib import ExitStack
+
+import concourse.mybir as mybir
+
+K, T, J, S, R, G, N = 1024, 1024, 384, 512, 512, 48, 256
+FLOPS = 2 * K * R * J + 2 * R * J * N
+
+F32 = mybir.dt.float32
+BF16 = mybir.dt.bfloat16
+I32 = mybir.dt.int32
+U32 = mybir.dt.uint32
+U16 = mybir.dt.uint16
+U8 = mybir.dt.uint8
+E4M3X4 = mybir.dt.float8_e4m3fn_x4
+E5M2X4 = mybir.dt.float8_e5m2_x4
+ALU = mybir.AluOpType
+ACT = mybir.ActivationFunctionType
+AXIS = mybir.AxisListType
+
+P = 128
+PACK = 4
+K_PASS = P * PACK
+PASSES = K // K_PASS
+CHUNK = 128
+CHUNKS = J // CHUNK
+BUNDLE = J // G
+LIST_COLS = CHUNK // 16
+RUN = 4
+VECTOR_SCALED = 5
+
+
+def tile_list_entryproducts_levelled_rowabove_kernel(
+    tc, xa, xb, fk, w_words, w_scales, wb_words, wb_scales, rs, offs, offs2, out
+):
+    nc = tc.nc
+    with ExitStack() as ctx:
+        keep = ctx.enter_context(tc.tile_pool(name="keep", bufs=1))
+        psum = ctx.enter_context(tc.psum_pool(name="psum", bufs=1))
+
+        list_a = keep.tile([P, J // 16], U16, name="list_a")
+        list_b = keep.tile([P, J // 16], U16, name="list_b")
+        factor = keep.tile([P, PASSES, PACK], F32, name="factor")
+        xa_rows = xa.rearrange("(z p t) c -> z p t c", p=P, t=PACK)
+        xb_rows = xb.rearrange("(z p t) c -> z p (t c)", p=P, t=PACK)
+        a_plane = [[keep.tile([P, T], F32, name=f"a_plane{z}{t}") for t in range(PACK)] for z in range(PASSES)]
+        b_pair = [[keep.tile([P, 2 * S], F32, name=f"b_pair{z}{h}") for h in range(2)] for z in range(PASSES)]
+        w_raw = [keep.tile([P, R], U32, name=f"w_raw{z}") for z in range(PASSES)]
+        w_code = [keep.tile([P, R], U32, name=f"w_code{z}", align_bytes=64) for z in range(PASSES)]
+        ws_raw = keep.tile([P, PASSES * R], U8, name="ws_raw")
+        w_scale = keep.tile([P, PASSES * R], U8, name="w_scale", align_bytes=64)
+        wb_code = keep.tile([P, N], U32, name="wb_code", align_bytes=64)
+        wb_scale = keep.tile([P, N], U8, name="wb_scale", align_bytes=64)
+        resid = keep.tile([P, CHUNKS, N], F32, name="resid")
+
+        def load_a(z, t):
+            nc.sync.dma_start(out=a_plane[z][t][:], in_=xa_rows[z, :, t, :])
+
+        def load_b(z, h):
+            nc.sync.dma_start(out=b_pair[z][h][:], in_=xb_rows[z, :, 2 * S * h : 2 * S * (h + 1)])
+
+        def load_w(z):
+            nc.sync.dma_start(
+                out=w_raw[z][:].bitcast(I32), in_=w_words[z].rearrange("p n t -> p (n t)").bitcast(I32)
+            )
+
+        nc.vector.memset(ws_raw[:].bitcast(U32), 0)
+        nc.vector.memset(wb_scale[:].bitcast(U32), 0)
+
+        def load_w_scales():
+            for r in range(4):
+                nc.sync.dma_start(
+                    out=ws_raw[r:P:32, :].bitcast(I32).rearrange("q (z c) -> q z c", z=PASSES),
+                    in_=w_scales.bitcast(I32)[:, r:16:4, :].rearrange("z q c -> q z c"),
+                )
+
+        def load_wb_scales():
+            for r in range(4):
+                nc.sync.dma_start(out=wb_scale[r:P:32, :].bitcast(I32), in_=wb_scales.bitcast(I32)[0, r:16:4, :])
+
+        load_b(0, 0)
+        nc.sync.dma_start(list_b[:], offs2)
+        nc.sync.dma_start(list_a[:], offs)
+        nc.sync.dma_start(out=factor[:], in_=fk.rearrange("(z p t) o -> p z (t o)", p=P, t=PACK))
+        load_a(0, 0)
+        load_a(0, 1)
+        load_w_scales()
+        load_b(0, 1)
+        load_b(1, 0)
+        load_a(0, 2)
+        load_a(0, 3)
+        load_b(1, 1)
+        load_a(1, 0)
+        load_a(1, 1)
+        load_w(0)
+        load_a(1, 2)
+        load_a(1, 3)
+        load_w(1)
+        nc.sync.dma_start(out=wb_code[:].bitcast(I32), in_=wb_words[0].rearrange("p n t -> p (n t)").bitcast(I32))
+        load_wb_scales()
+        nc.sync.dma_start(out=resid[:], in_=rs.rearrange("(c p) n -> p c n", p=P))
+
+        prod = [keep.tile([P, PACK, J], F32, name=f"prod{z}") for z in range(PASSES)]
+        acc = [psum.tile([P, PACK, CHUNK], F32, name=f"acc{c}") for c in range(CHUNKS)]
+
+        def scaled_b(z, t):
+            picked = keep.tile([P, J], F32, name=f"picked{z}{t}")
+            scaled = keep.tile([P, J], F32, name=f"scaled{z}{t}")
+            pair = b_pair[z][t // 2]
+            if (z, t) == (0, 0):
+                nc.vector.tensor_copy(picked[:], pair[:].indirect(list_b[:]))
+            elif t % 2 == 0:
+                nc.scalar.activation(picked[:], pair[:].indirect(list_b[:]), ACT.Copy)
+            else:
+                for lo, hi in ((0, 256), (256, J)):
+                    nc.scalar.activation(
+                        picked[:, lo:hi], pair[:, S:].indirect(list_b[:, lo // 16 : hi // 16]), ACT.Copy
+                    )
+            if PACK * z + t < VECTOR_SCALED:
+                nc.vector.tensor_scalar(scaled[:], picked[:], factor[:, z, t : t + 1], None, ALU.mult)
+            else:
+                nc.scalar.activation(scaled[:], picked[:], ACT.Copy, scale=factor[:, z, t : t + 1])
+            return scaled
+
+        def product(z, t, scaled, lo, hi):
+            nc.vector.tensor_tensor(
+                prod[z][:, t, lo:hi],
+                a_plane[z][t][:].indirect(list_a[:, lo // 16 : hi // 16]),
+                scaled[:, lo:hi],
+                ALU.mult,
+            )
+
+        def interleave(z, lo, hi, copy):
+            grouped = keep.tile([P, hi - lo, PACK], BF16, name=f"u_grouped{z}_{lo}", align_bytes=64)
+            copy(
+                out=grouped[:].rearrange("p (c i) t -> p c t i", i=RUN),
+                in_=prod[z][:, :, lo:hi].rearrange("p t (c i) -> p c t i", i=RUN),
+            )
+            return grouped
+
+        def quantize(grouped, name):
+            width = grouped.shape[1]
+            code = keep.tile([P, width], U32, name=f"{name}_code", align_bytes=64)
+            scale = keep.tile([P, width], U8, name=f"{name}_scale", align_bytes=64)
+            nc.vector.quantize_mx(
+                out=code[:].bitcast(E4M3X4), scales=scale[:], in_=grouped[:].rearrange("p j t -> p (j t)")
+            )
+            return code, scale
+
+        def order_w(z):
+            nc.scalar.copy(
+                out=w_code[z][:].rearrange("p (t m) -> p t m", t=PACK),
+                in_=w_raw[z][:].rearrange("p (m t) -> p t m", t=PACK),
+            )
+
+        def first_matmuls(z, c, code, scale):
+            for t in range(PACK):
+                nc.tensor.matmul_mx(
+                    out=acc[c][:, t, :],
+                    lhsT=w_code[z][:, P * t : P * (t + 1)].bitcast(E5M2X4),
+                    lhsT_scale=w_scale[:, R * z + P * t : R * z + P * (t + 1)],
+                    rhs=code.bitcast(E4M3X4),
+                    rhs_scale=scale,
+                    start=(z == 0 and t == 0),
+                    stop=(z == PASSES - 1 and t == PACK - 1),
+                )
+
+        for t in range(PACK):
+            product(0, t, scaled_b(0, t), 0, J)
+            if t == 1:
+                nc.vector.tensor_copy(
+                    out=w_scale[:].rearrange("p (z t m) -> p z t m", z=PASSES, t=PACK),
+                    in_=ws_raw[:].rearrange("p (z m t) -> p z t m", z=PASSES, t=PACK),
+                )
+        code0, scale0 = quantize(interleave(0, 0, J, nc.vector.tensor_copy), "u0")
+
+        for t in range(PACK - 1):
+            product(1, t, scaled_b(1, t), 0, J)
+        order_w(0)
+        last_scaled = scaled_b(1, PACK - 1)
+        for c in range(CHUNKS):
+            cols = slice(CHUNK * c, CHUNK * (c + 1))
+            first_matmuls(0, c, code0[:, cols], scale0[:, cols])
+        order_w(1)
+        for c in range(CHUNKS):
+            lo, hi = CHUNK * c, CHUNK * (c + 1)
+            product(1, PACK - 1, last_scaled, lo, hi)
+            code, scale = quantize(interleave(1, lo, hi, nc.scalar.copy if c == CHUNKS - 1 else nc.vector.tensor_copy), f"u1_{c}")
+            first_matmuls(1, c, code[:], scale[:])
+
+        bundles = CHUNK // BUNDLE
+        second = []
+        for c in range(CHUNKS):
+            total = keep.tile([P, bundles, PACK], F32, name=f"total{c}")
+            mean = keep.tile([P, bundles, PACK], F32, name=f"mean{c}")
+            nc.vector.tensor_reduce(
+                out=total[:], in_=acc[c][:].rearrange("p t (g i) -> p g t i", i=BUNDLE), axis=AXIS.X, op=ALU.add
+            )
+            nc.vector.tensor_scalar(mean[:], total[:], 1.0 / BUNDLE, None, ALU.mult)
+            hid = keep.tile([P, CHUNK, PACK], BF16, name=f"hid{c}", align_bytes=64)
+            nc.vector.tensor_tensor(
+                hid[:].rearrange("p (g i) t -> p g i t", i=BUNDLE),
+                acc[c][:].rearrange("p t (g i) -> p g i t", i=BUNDLE),
+                mean[:].unsqueeze(2).to_broadcast([P, bundles, BUNDLE, PACK]),
+                ALU.subtract,
+            )
+            code, scale = quantize(hid, f"hid{c}")
+            scores = psum.tile([P, N], F32, name=f"scores{c}")
+            nc.tensor.matmul_mx(
+                out=scores[:],
+                lhsT=code[:].bitcast(E4M3X4),
+                lhsT_scale=scale[:],
+                rhs=wb_code[:].bitcast(E5M2X4),
+                rhs_scale=wb_scale[:],
+                start=True,
+                stop=True,
+            )
+            magnitude = keep.tile([P, N], F32, name=f"magnitude{c}")
+            level = keep.tile([P, 1], F32, name=f"level{c}")
+            nc.scalar.activation(magnitude[:], scores[:], ACT.Abs, scale=1.0 / N, accum_out=level[:])
+            taken = keep.tile([P, N], F32, name=f"taken{c}")
+            nc.scalar.activation(taken[:], resid[:, c, :], ACT.Identity, bias=level[:], scale=0.3)
+            second.append((scores, level, taken))
+
+        for c, (scores, level, taken) in enumerate(second):
+            result = keep.tile([P, N], F32, name=f"result{c}")
+            nc.vector.scalar_tensor_tensor(result[:], scores[:], level[:], taken[:], ALU.max, ALU.subtract)
+            nc.sync.dma_start(out=out[CHUNK * c : CHUNK * (c + 1), :], in_=result[:])

@@ -82,9 +82,9 @@ def tile_list_entryproducts_levelled_rowabove_kernel(
         nc.sync.dma_start(list_a[:], offs)
         nc.sync.dma_start(out=factor[:], in_=fk.rearrange("(z p t) o -> p z (t o)", p=P, t=PACK))
         load_a(0, 0)
-        load_a(0, 1)
-        load_w_scales()
         load_b(0, 1)
+        load_w_scales()
+        load_a(0, 1)
         load_b(1, 0)
         load_a(0, 2)
         load_a(0, 3)
@@ -187,24 +187,8 @@ def tile_list_entryproducts_levelled_rowabove_kernel(
             code, scale = quantize(interleave(1, lo, hi, nc.scalar.copy if c == CHUNKS - 1 else nc.vector.tensor_copy), f"u1_{c}")
             first_matmuls(1, c, code[:], scale[:])
 
-        bundles = CHUNK // BUNDLE
-        second = []
-        for c in range(CHUNKS):
-            total = keep.tile([P, bundles, PACK], F32, name=f"total{c}")
-            mean = keep.tile([P, bundles, PACK], F32, name=f"mean{c}")
-            nc.vector.tensor_reduce(
-                out=total[:], in_=acc[c][:].rearrange("p t (g i) -> p g t i", i=BUNDLE), axis=AXIS.X, op=ALU.add
-            )
-            nc.vector.tensor_scalar(mean[:], total[:], 1.0 / BUNDLE, None, ALU.mult)
-            hid = keep.tile([P, CHUNK, PACK], BF16, name=f"hid{c}", align_bytes=64)
-            nc.vector.tensor_tensor(
-                hid[:].rearrange("p (g i) t -> p g i t", i=BUNDLE),
-                acc[c][:].rearrange("p t (g i) -> p g i t", i=BUNDLE),
-                mean[:].unsqueeze(2).to_broadcast([P, bundles, BUNDLE, PACK]),
-                ALU.subtract,
-            )
-            code, scale = quantize(hid, f"hid{c}")
-            scores = psum.tile([P, N], F32, name=f"scores{c}")
+        def second_matmul(code, scale, name):
+            scores = psum.tile([P, N], F32, name=name)
             nc.tensor.matmul_mx(
                 out=scores[:],
                 lhsT=code[:].bitcast(E4M3X4),
@@ -214,14 +198,42 @@ def tile_list_entryproducts_levelled_rowabove_kernel(
                 start=True,
                 stop=True,
             )
+            return scores
+
+        floor = keep.tile([P, N], F32, name="floor")
+        nc.scalar.activation(floor[:], resid[:, CHUNKS - 1, :], ACT.Copy, scale=-0.3)
+        bundles = CHUNK // BUNDLE
+        second = []
+        for c in range(CHUNKS):
+            total = keep.tile([P, bundles, PACK], F32, name=f"total{c}")
+            mean = keep.tile([P, bundles, PACK], F32, name=f"mean{c}")
+            nc.vector.tensor_reduce(
+                out=total[:], in_=acc[c][:].rearrange("p t (g i) -> p g t i", i=BUNDLE), axis=AXIS.X, op=ALU.add
+            )
+            nc.scalar.activation(mean[:], total[:], ACT.Copy, scale=1.0 / BUNDLE)
+            hid = keep.tile([P, CHUNK, PACK], BF16, name=f"hid{c}", align_bytes=64)
+            nc.vector.tensor_tensor(
+                hid[:].rearrange("p (g i) t -> p g i t", i=BUNDLE),
+                acc[c][:].rearrange("p t (g i) -> p g i t", i=BUNDLE),
+                mean[:].unsqueeze(2).to_broadcast([P, bundles, BUNDLE, PACK]),
+                ALU.subtract,
+            )
+            code, scale = quantize(hid, f"hid{c}")
+            scores = second_matmul(code, scale, f"scores{c}")
             magnitude = keep.tile([P, N], F32, name=f"magnitude{c}")
             level = keep.tile([P, 1], F32, name=f"level{c}")
             nc.scalar.activation(magnitude[:], scores[:], ACT.Abs, scale=1.0 / N, accum_out=level[:])
-            taken = keep.tile([P, N], F32, name=f"taken{c}")
-            nc.scalar.activation(taken[:], resid[:, c, :], ACT.Identity, bias=level[:], scale=0.3)
-            second.append((scores, level, taken))
+            if c < CHUNKS - 1:
+                taken = keep.tile([P, N], F32, name=f"taken{c}")
+                nc.scalar.activation(taken[:], resid[:, c, :], ACT.Identity, bias=level[:], scale=0.3)
+                second.append((scores, level[:], taken, ALU.max, taken, ALU.subtract))
+            else:
+                again = second_matmul(code, scale, "scores_again")
+                shifted = keep.tile([P, N], F32, name="shifted")
+                nc.vector.tensor_tensor(shifted[:], again[:], floor[:], ALU.add)
+                second.append((shifted, level[:], floor, ALU.subtract, floor, ALU.max))
 
-        for c, (scores, level, taken) in enumerate(second):
+        for c, (values, level, other, op0, unused, op1) in enumerate(second):
             result = keep.tile([P, N], F32, name=f"result{c}")
-            nc.vector.scalar_tensor_tensor(result[:], scores[:], level[:], taken[:], ALU.max, ALU.subtract)
+            nc.vector.scalar_tensor_tensor(result[:], values[:], level, other[:], op0, op1)
             nc.sync.dma_start(out=out[CHUNK * c : CHUNK * (c + 1), :], in_=result[:])

@@ -26,7 +26,7 @@ CHUNKS = J // CHUNK
 BUNDLE = J // G
 LIST_COLS = CHUNK // 16
 RUN = 4
-VECTOR_SCALED = 5
+VECTOR_SCALED = 4
 
 
 def tile_list_entryproducts_levelled_rowabove_kernel(
@@ -44,8 +44,10 @@ def tile_list_entryproducts_levelled_rowabove_kernel(
         xb_rows = xb.rearrange("(z p t) c -> z p (t c)", p=P, t=PACK)
         a_plane = [[keep.tile([P, T], F32, name=f"a_plane{z}{t}") for t in range(PACK)] for z in range(PASSES)]
         b_pair = [[keep.tile([P, 2 * S], F32, name=f"b_pair{z}{h}") for h in range(2)] for z in range(PASSES)]
-        w_raw = [keep.tile([P, R], U32, name=f"w_raw{z}") for z in range(PASSES)]
-        w_code = [keep.tile([P, R], U32, name=f"w_code{z}", align_bytes=64) for z in range(PASSES)]
+        w_raw = [keep.tile([P, R], U32, name=f"w_raw{z}", tag=f"w_raw{z}", align_bytes=64) for z in range(PASSES)]
+        w_code = [
+            [keep.tile([P, 2, P], U32, name=f"w_code{z}{h}", align_bytes=64) for h in range(2)] for z in range(PASSES)
+        ]
         ws_raw = keep.tile([P, PASSES * R], U8, name="ws_raw")
         w_scale = keep.tile([P, PASSES * R], U8, name="w_scale", align_bytes=64)
         wb_code = keep.tile([P, N], U32, name="wb_code", align_bytes=64)
@@ -85,21 +87,21 @@ def tile_list_entryproducts_levelled_rowabove_kernel(
         load_b(0, 1)
         load_w_scales()
         load_a(0, 1)
-        load_b(1, 0)
         load_a(0, 2)
+        load_b(1, 0)
         load_a(0, 3)
         load_b(1, 1)
         load_a(1, 0)
         load_a(1, 1)
-        load_w(0)
         load_a(1, 2)
         load_a(1, 3)
+        load_w(0)
         load_w(1)
         nc.sync.dma_start(out=wb_code[:].bitcast(I32), in_=wb_words[0].rearrange("p n t -> p (n t)").bitcast(I32))
         load_wb_scales()
         nc.sync.dma_start(out=resid[:], in_=rs.rearrange("(c p) n -> p c n", p=P))
 
-        prod = [keep.tile([P, PACK, J], F32, name=f"prod{z}") for z in range(PASSES)]
+        prod = [keep.tile([P, PACK, J], F32, name=f"prod{z}", tag=f"prod{z}") for z in range(PASSES)]
         acc = [psum.tile([P, PACK, CHUNK], F32, name=f"acc{c}") for c in range(CHUNKS)]
 
         def scaled_b(z, t):
@@ -129,8 +131,8 @@ def tile_list_entryproducts_levelled_rowabove_kernel(
                 ALU.mult,
             )
 
-        def interleave(z, lo, hi, copy):
-            grouped = keep.tile([P, hi - lo, PACK], BF16, name=f"u_grouped{z}_{lo}", align_bytes=64)
+        def interleave(z, lo, hi, copy, tag=""):
+            grouped = keep.tile([P, hi - lo, PACK], BF16, name=f"u_grouped{z}_{lo}", tag=tag, align_bytes=64)
             copy(
                 out=grouped[:].rearrange("p (c i) t -> p c t i", i=RUN),
                 in_=prod[z][:, :, lo:hi].rearrange("p t (c i) -> p c t i", i=RUN),
@@ -147,21 +149,22 @@ def tile_list_entryproducts_levelled_rowabove_kernel(
             return code, scale
 
         def order_w(z):
-            nc.scalar.copy(
-                out=w_code[z][:].rearrange("p (t m) -> p t m", t=PACK),
-                in_=w_raw[z][:].rearrange("p (m t) -> p t m", t=PACK),
-            )
+            for lo in (0, 2):
+                nc.scalar.copy(
+                    out=w_code[z][lo // 2][:].rearrange("p t (c i) -> p c t i", i=RUN),
+                    in_=w_raw[z][:].rearrange("p (c i t) -> p c t i", t=PACK, i=RUN)[:, :, lo : lo + 2, :],
+                )
 
-        def first_matmuls(z, c, code, scale):
+        def first_matmuls(z, c, code, scale, opens):
             for t in range(PACK):
                 nc.tensor.matmul_mx(
                     out=acc[c][:, t, :],
-                    lhsT=w_code[z][:, P * t : P * (t + 1)].bitcast(E5M2X4),
+                    lhsT=w_code[z][t // 2][:, t % 2, :].bitcast(E5M2X4),
                     lhsT_scale=w_scale[:, R * z + P * t : R * z + P * (t + 1)],
                     rhs=code.bitcast(E4M3X4),
                     rhs_scale=scale,
-                    start=(z == 0 and t == 0),
-                    stop=(z == PASSES - 1 and t == PACK - 1),
+                    start=(opens and t == 0),
+                    stop=(not opens and t == PACK - 1),
                 )
 
         for t in range(PACK):
@@ -175,17 +178,18 @@ def tile_list_entryproducts_levelled_rowabove_kernel(
 
         for t in range(PACK - 1):
             product(1, t, scaled_b(1, t), 0, J)
-        order_w(0)
         last_scaled = scaled_b(1, PACK - 1)
-        for c in range(CHUNKS):
-            cols = slice(CHUNK * c, CHUNK * (c + 1))
-            first_matmuls(0, c, code0[:, cols], scale0[:, cols])
+        order_w(0)
         order_w(1)
         for c in range(CHUNKS):
             lo, hi = CHUNK * c, CHUNK * (c + 1)
             product(1, PACK - 1, last_scaled, lo, hi)
-            code, scale = quantize(interleave(1, lo, hi, nc.scalar.copy if c == CHUNKS - 1 else nc.vector.tensor_copy), f"u1_{c}")
-            first_matmuls(1, c, code[:], scale[:])
+            code, scale = quantize(interleave(1, lo, hi, nc.scalar.copy if c == CHUNKS - 1 else nc.vector.tensor_copy, "w_raw1" if c == CHUNKS - 1 else ""), f"u1_{c}")
+            if c == 0:
+                first_matmuls(0, c, code0[:, lo:hi], scale0[:, lo:hi], True)
+            first_matmuls(1, c, code[:], scale[:], c > 0)
+            if c > 0:
+                first_matmuls(0, c, code0[:, lo:hi], scale0[:, lo:hi], False)
 
         def second_matmul(code, scale, name):
             scores = psum.tile([P, N], F32, name=name)
@@ -200,7 +204,7 @@ def tile_list_entryproducts_levelled_rowabove_kernel(
             )
             return scores
 
-        floor = keep.tile([P, N], F32, name="floor")
+        floor = keep.tile([P, N], F32, name="floor", tag=f"prod{PASSES - 1}")
         nc.scalar.activation(floor[:], resid[:, CHUNKS - 1, :], ACT.Copy, scale=-0.3)
         bundles = CHUNK // BUNDLE
         second = []

from contextlib import ExitStack

import concourse.mybir as mybir

K, T, J, S, R, G, N = 1024, 1024, 384, 512, 512, 48, 256
FLOPS = 2 * K * R * J + 2 * R * J * N

F32 = mybir.dt.float32
BF16 = mybir.dt.bfloat16
I32 = mybir.dt.int32
U32 = mybir.dt.uint32
U16 = mybir.dt.uint16
U8 = mybir.dt.uint8
E4M3X4 = mybir.dt.float8_e4m3fn_x4
E5M2X4 = mybir.dt.float8_e5m2_x4
ALU = mybir.AluOpType
ACT = mybir.ActivationFunctionType
AXIS = mybir.AxisListType

P = 128
PACK = 4
K_PASS = P * PACK
PASSES = K // K_PASS
CHUNK = 128
CHUNKS = J // CHUNK
BUNDLE = J // G
LIST_COLS = CHUNK // 16
RUN = 4
VECTOR_SCALED = 4


def tile_list_entryproducts_levelled_rowabove_kernel(
    tc, xa, xb, fk, w_words, w_scales, wb_words, wb_scales, rs, offs, offs2, out
):
    nc = tc.nc
    with ExitStack() as ctx:
        keep = ctx.enter_context(tc.tile_pool(name="keep", bufs=1))
        psum = ctx.enter_context(tc.psum_pool(name="psum", bufs=1))

        list_a = keep.tile([P, J // 16], U16, name="list_a")
        list_b = keep.tile([P, J // 16], U16, name="list_b")
        factor = keep.tile([P, PASSES, PACK], F32, name="factor")
        xa_rows = xa.rearrange("(z p t) c -> z p t c", p=P, t=PACK)
        xb_rows = xb.rearrange("(z p t) c -> z p (t c)", p=P, t=PACK)
        a_plane = [[keep.tile([P, T], F32, name=f"a_plane{z}{t}") for t in range(PACK)] for z in range(PASSES)]
        b_pair = [[keep.tile([P, 2 * S], F32, name=f"b_pair{z}{h}") for h in range(2)] for z in range(PASSES)]
        w_raw = [keep.tile([P, R], U32, name=f"w_raw{z}", tag=f"w_raw{z}", align_bytes=64) for z in range(PASSES)]
        w_code = [
            [keep.tile([P, 2, P], U32, name=f"w_code{z}{h}", align_bytes=64) for h in range(2)] for z in range(PASSES)
        ]
        ws_raw = keep.tile([P, PASSES * R], U8, name="ws_raw")
        w_scale = keep.tile([P, PASSES * R], U8, name="w_scale", align_bytes=64)
        wb_code = keep.tile([P, N], U32, name="wb_code", align_bytes=64)
        wb_scale = keep.tile([P, N], U8, name="wb_scale", align_bytes=64)
        resid = keep.tile([P, CHUNKS, N], F32, name="resid")

        def load_a(z, t):
            nc.sync.dma_start(out=a_plane[z][t][:], in_=xa_rows[z, :, t, :])

        def load_b(z, h):
            nc.sync.dma_start(out=b_pair[z][h][:], in_=xb_rows[z, :, 2 * S * h : 2 * S * (h + 1)])

        def load_w(z):
            nc.sync.dma_start(
                out=w_raw[z][:].bitcast(I32), in_=w_words[z].rearrange("p n t -> p (n t)").bitcast(I32)
            )

        nc.vector.memset(ws_raw[:].bitcast(U32), 0)
        nc.vector.memset(wb_scale[:].bitcast(U32), 0)

        def load_w_scales():
            for r in range(4):
                nc.sync.dma_start(
                    out=ws_raw[r:P:32, :].bitcast(I32).rearrange("q (z c) -> q z c", z=PASSES),
                    in_=w_scales.bitcast(I32)[:, r:16:4, :].rearrange("z q c -> q z c"),
                )

        def load_wb_scales():
            for r in range(4):
                nc.sync.dma_start(out=wb_scale[r:P:32, :].bitcast(I32), in_=wb_scales.bitcast(I32)[0, r:16:4, :])

        load_b(0, 0)
        nc.sync.dma_start(list_b[:], offs2)
        nc.sync.dma_start(list_a[:], offs)
        nc.sync.dma_start(out=factor[:], in_=fk.rearrange("(z p t) o -> p z (t o)", p=P, t=PACK))
        load_a(0, 0)
        load_b(0, 1)
        load_w_scales()
        load_a(0, 1)
        load_a(0, 2)
        load_b(1, 0)
        load_a(0, 3)
        load_b(1, 1)
        load_a(1, 0)
        load_a(1, 1)
        load_a(1, 2)
        load_a(1, 3)
        load_w(0)
        load_w(1)
        nc.sync.dma_start(out=wb_code[:].bitcast(I32), in_=wb_words[0].rearrange("p n t -> p (n t)").bitcast(I32))
        load_wb_scales()
        nc.sync.dma_start(out=resid[:], in_=rs.rearrange("(c p) n -> p c n", p=P))

        prod = [keep.tile([P, PACK, J], F32, name=f"prod{z}", tag=f"prod{z}") for z in range(PASSES)]
        acc = [psum.tile([P, PACK, CHUNK], F32, name=f"acc{c}") for c in range(CHUNKS)]

        def scaled_b(z, t):
            picked = keep.tile([P, J], F32, name=f"picked{z}{t}")
            scaled = keep.tile([P, J], F32, name=f"scaled{z}{t}")
            pair = b_pair[z][t // 2]
            if (z, t) == (0, 0):
                nc.vector.tensor_copy(picked[:], pair[:].indirect(list_b[:]))
            elif t % 2 == 0:
                nc.scalar.activation(picked[:], pair[:].indirect(list_b[:]), ACT.Copy)
            else:
                for lo, hi in ((0, 256), (256, J)):
                    nc.scalar.activation(
                        picked[:, lo:hi], pair[:, S:].indirect(list_b[:, lo // 16 : hi // 16]), ACT.Copy
                    )
            if PACK * z + t < VECTOR_SCALED:
                nc.vector.tensor_scalar(scaled[:], picked[:], factor[:, z, t : t + 1], None, ALU.mult)
            else:
                nc.scalar.activation(scaled[:], picked[:], ACT.Copy, scale=factor[:, z, t : t + 1])
            return scaled

        def product(z, t, scaled, lo, hi):
            nc.vector.tensor_tensor(
                prod[z][:, t, lo:hi],
                a_plane[z][t][:].indirect(list_a[:, lo // 16 : hi // 16]),
                scaled[:, lo:hi],
                ALU.mult,
            )

        def interleave(z, lo, hi, copy, tag=""):
            grouped = keep.tile([P, hi - lo, PACK], BF16, name=f"u_grouped{z}_{lo}", tag=tag, align_bytes=64)
            copy(
                out=grouped[:].rearrange("p (c i) t -> p c t i", i=RUN),
                in_=prod[z][:, :, lo:hi].rearrange("p t (c i) -> p c t i", i=RUN),
            )
            return grouped

        def quantize(grouped, name):
            width = grouped.shape[1]
            code = keep.tile([P, width], U32, name=f"{name}_code", align_bytes=64)
            scale = keep.tile([P, width], U8, name=f"{name}_scale", align_bytes=64)
            nc.vector.quantize_mx(
                out=code[:].bitcast(E4M3X4), scales=scale[:], in_=grouped[:].rearrange("p j t -> p (j t)")
            )
            return code, scale

        def order_w(z):
            for lo in (0, 2):
                nc.scalar.copy(
                    out=w_code[z][lo // 2][:].rearrange("p t (c i) -> p c t i", i=RUN),
                    in_=w_raw[z][:].rearrange("p (c i t) -> p c t i", t=PACK, i=RUN)[:, :, lo : lo + 2, :],
                )

        def first_matmuls(z, c, code, scale, opens):
            for t in range(PACK):
                nc.tensor.matmul_mx(
                    out=acc[c][:, t, :],
                    lhsT=w_code[z][t // 2][:, t % 2, :].bitcast(E5M2X4),
                    lhsT_scale=w_scale[:, R * z + P * t : R * z + P * (t + 1)],
                    rhs=code.bitcast(E4M3X4),
                    rhs_scale=scale,
                    start=(opens and t == 0),
                    stop=(not opens and t == PACK - 1),
                )

        for t in range(PACK):
            product(0, t, scaled_b(0, t), 0, J)
            if t == 1:
                nc.vector.tensor_copy(
                    out=w_scale[:].rearrange("p (z t m) -> p z t m", z=PASSES, t=PACK),
                    in_=ws_raw[:].rearrange("p (z m t) -> p z t m", z=PASSES, t=PACK),
                )
        code0, scale0 = quantize(interleave(0, 0, J, nc.vector.tensor_copy), "u0")

        for t in range(PACK - 1):
            product(1, t, scaled_b(1, t), 0, J)
        last_scaled = scaled_b(1, PACK - 1)
        order_w(0)
        order_w(1)
        for c in range(CHUNKS):
            lo, hi = CHUNK * c, CHUNK * (c + 1)
            product(1, PACK - 1, last_scaled, lo, hi)
            code, scale = quantize(interleave(1, lo, hi, nc.scalar.copy if c == CHUNKS - 1 else nc.vector.tensor_copy, "w_raw1" if c == CHUNKS - 1 else ""), f"u1_{c}")
            if c == 0:
                first_matmuls(0, c, code0[:, lo:hi], scale0[:, lo:hi], True)
            first_matmuls(1, c, code[:], scale[:], c > 0)
            if c > 0:
                first_matmuls(0, c, code0[:, lo:hi], scale0[:, lo:hi], False)

        def second_matmul(code, scale, name):
            scores = psum.tile([P, N], F32, name=name)
            nc.tensor.matmul_mx(
                out=scores[:],
                lhsT=code[:].bitcast(E4M3X4),
                lhsT_scale=scale[:],
                rhs=wb_code[:].bitcast(E5M2X4),
                rhs_scale=wb_scale[:],
                start=True,
                stop=True,
            )
            return scores

        floor = keep.tile([P, N], F32, name="floor", tag=f"prod{PASSES - 1}")
        nc.scalar.activation(floor[:], resid[:, CHUNKS - 1, :], ACT.Copy, scale=-0.3)
        bundles = CHUNK // BUNDLE
        second = []
        for c in range(CHUNKS):
            total = keep.tile([P, bundles, PACK], F32, name=f"total{c}")
            mean = keep.tile([P, bundles, PACK], F32, name=f"mean{c}")
            nc.vector.tensor_reduce(
                out=total[:], in_=acc[c][:].rearrange("p t (g i) -> p g t i", i=BUNDLE), axis=AXIS.X, op=ALU.add
            )
            nc.scalar.activation(mean[:], total[:], ACT.Copy, scale=1.0 / BUNDLE)
            hid = keep.tile([P, CHUNK, PACK], BF16, name=f"hid{c}", align_bytes=64)
            nc.vector.tensor_tensor(
                hid[:].rearrange("p (g i) t -> p g i t", i=BUNDLE),
                acc[c][:].rearrange("p t (g i) -> p g i t", i=BUNDLE),
                mean[:].unsqueeze(2).to_broadcast([P, bundles, BUNDLE, PACK]),
                ALU.subtract,
            )
            code, scale = quantize(hid, f"hid{c}")
            scores = second_matmul(code, scale, f"scores{c}")
            magnitude = keep.tile([P, N], F32, name=f"magnitude{c}")
            level = keep.tile([P, 1], F32, name=f"level{c}")
            nc.scalar.activation(magnitude[:], scores[:], ACT.Abs, scale=1.0 / N, accum_out=level[:])
            if c < CHUNKS - 1:
                taken = keep.tile([P, N], F32, name=f"taken{c}")
                nc.scalar.activation(taken[:], resid[:, c, :], ACT.Identity, bias=level[:], scale=0.3)
                second.append((scores, level[:], taken, ALU.max, taken, ALU.subtract))
            else:
                again = second_matmul(code, scale, "scores_again")
                shifted = keep.tile([P, N], F32, name="shifted")
                nc.vector.tensor_tensor(shifted[:], again[:], floor[:], ALU.add)
                second.append((shifted, level[:], floor, ALU.subtract, floor, ALU.max))

        for c, (values, level, other, op0, unused, op1) in enumerate(second):
            result = keep.tile([P, N], F32, name=f"result{c}")
            nc.vector.scalar_tensor_tensor(result[:], values[:], level, other[:], op0, op1)
            nc.sync.dma_start(out=out[CHUNK * c : CHUNK * (c + 1), :], in_=result[:])
